import numpy as np, ml_dtypes
CORES = [37,45,53,61,69,109,117,125]
N = 8
import mx_ref
NC, KT, ROOT = 256, 2, 6
BF = ml_dtypes.bfloat16
def setup_inputs(rng):
    def f(*shape):
        return mx_ref.flush((rng.standard_normal(shape, dtype=np.float32) * np.exp2(rng.integers(-2, 3, shape[:-1] + (1,)))).astype(BF))
    return {"w": f(N, 128, KT * 512), "x": f(N, 128, KT * 4 * NC)}
def setup_inputs_blocks(rng):
    d = setup_inputs(rng)
    for k in ("w", "x"): d[k] = mx_ref.spread(d[k], rng, 4)
    return d
def setup_inputs_wide(rng):
    d = setup_inputs(rng)
    for k in ("w", "x"): d[k] = mx_ref.flush((d[k].astype(np.float32) * np.exp2(rng.integers(-8, 9, (N, 1, 1))).astype(np.float32)).astype(BF))
    return d
def setup_inputs_zeros(rng):
    d = setup_inputs(rng); v = d["x"].reshape(N, 128, -1, 4).copy()
    v[np.broadcast_to((rng.random((N, 1, v.shape[2], 1)) < 0.33), v.shape)] = 0
    d["x"] = v.reshape(d["x"].shape)
    return d
def reference(w, x):
    QW = [mx_ref.quantize(w[ROOT][:, 512 * t:512 * t + 512]) for t in range(KT)]
    y = np.zeros((N, 128, NC), np.float32)
    for r in range(N):
        for t in range(KT):
            p = mx_ref.matmul(QW[t], mx_ref.quantize(x[r][:, 4 * NC * t:4 * NC * t + 4 * NC]))
            y[r] = p if t == 0 else y[r] + p
    return {"y": y}

@@ -1,0 +1,154 @@
+from concourse.bass import DstId, RemoteDMATransfer
+from concourse.mybir import dt
+
+KT = 2
+WCOL = 128
+XCOL = 256
+
+SCRATCH = {
+    "wb": ("sbuf", [128, KT * 4 * WCOL], "bfloat16"),
+    "xb": ("sbuf", [128, KT * 4 * XCOL], "bfloat16"),
+    "wq": ("sbuf", [128, KT * WCOL], "float8_e4m3fn_x4"),
+    "ws": ("sbuf", [128, KT * WCOL], "uint8"),
+    "xq": ("sbuf", [128, KT * XCOL], "float8_e4m3fn_x4"),
+    "xs": ("sbuf", [128, KT * XCOL], "uint8"),
+    "acc": ("psum", [128, 512], "float32"),
+    "yb": ("sbuf", [128, XCOL], "float32"),
+}
+SEMAPHORES = ["w0", "w1", "x0", "x1", "qw", "qx", "arr", "sent", "mm", "cp", "st"]
+
+
+def _engines(mask):
+    return [e for e in range(mask.bit_length()) if (mask >> e) & 1]
+
+
+def _mask(engines):
+    m = 0
+    for e in engines:
+        m |= 1 << e
+    return m
+
+
+def _plan(cores, root_rank, topo):
+    root = cores[root_rank]
+    dests = [c for c in cores if c != root]
+    near = [d for d in dests if topo.may_write(root, d)]
+    far = [d for d in dests if not topo.may_write(root, d)]
+    chipmates = [c for c in range(topo.CHIPS * topo.CORES_PER_CHIP)
+                 if topo.chip(c) == topo.chip(root) and c != root and c not in cores]
+    owners = [c for c in chipmates if all(topo.may_write(c, d) for d in far)]
+    own_same = [c for c in owners if topo.die(c) == topo.die(root)]
+    own_other = [c for c in owners if topo.die(c) != topo.die(root)]
+    plain_other = [c for c in chipmates if c not in owners and topo.die(c) != topo.die(root)]
+    half = len(far) // 2
+    far_a, far_b = far[:half], far[half:]
+    return {
+        "root": root, "near": near,
+        "c_same": own_same[0], "c_other": own_other[0],
+        "s_same": own_same[1], "s_other": own_other[1],
+        "s_near": plain_other[0],
+        "jobs": {
+            own_same[0]: ("C", far_a), own_other[0]: ("C", far_b),
+            own_same[1]: ("S", far_b), own_other[1]: ("S", far_a),
+            plain_other[0]: ("S", near),
+        },
+    }
+
+
+def rank_program(g, core, T, topo):
+    plan = _plan(T.cores, T.root, topo)
+    root = plan["root"]
+    rank = T.rank_of(core)
+
+    def piece(kind):
+        if kind == "C":
+            return T.wq[:, 0:KT * WCOL].bitcast(dt.uint8)
+        return T.ws[:, 0:KT * WCOL]
+
+    def transfer(kind, dsts, engines):
+        ids = []
+        for d in dsts:
+            rid, pid, _ = topo.addr(d)
+            ids.append(DstId(rid=rid, pnc=pid))
+        return RemoteDMATransfer(dst_ids=ids, dma_engine_mask=_mask(engines), remote_sem=T.sem.arr,
+                                 srcs=[piece(kind)], dsts=[piece(kind) for _ in dsts])
+
+    def common(src, dsts):
+        m = topo.mask(src, dsts[0])
+        for d in dsts[1:]:
+            m &= topo.mask(src, d)
+        return _engines(m)
+
+    if core in plan["jobs"]:
+        kind, dsts = plan["jobs"][core]
+        eng = common(core, dsts)
+        g.wait_ge(T.sem.arr, _landing(plan, topo)[core])
+        g.remote_dma_fused([transfer(kind, dsts, eng)], local_sem=T.sem.sent)
+        g.wait_ge(T.sem.sent, len(eng))
+        return
+    if rank is None:
+        return
+
+    if core == root:
+        g.sync.dma_start(T.wb[:, 0:4 * WCOL], T.w[:, 0:4 * WCOL]).then_inc(T.sem.w0, 16)
+        g.scalar.dma_start(T.wb[:, 4 * WCOL:8 * WCOL], T.w[:, 4 * WCOL:8 * WCOL]).then_inc(T.sem.w1, 16)
+    g.sync.dma_start(T.xb[:, 0:4 * XCOL], T.x[:, 0:4 * XCOL]).then_inc(T.sem.x0, 16)
+    g.scalar.dma_start(T.xb[:, 4 * XCOL:8 * XCOL], T.x[:, 4 * XCOL:8 * XCOL]).then_inc(T.sem.x1, 16)
+
+    if core == root:
+        for t, sem in enumerate((T.sem.w0, T.sem.w1)):
+            g.vector.wait_ge(sem, 16)
+            g.vector.quantize_mx(T.wq[:, t * WCOL:(t + 1) * WCOL], T.ws[:, t * WCOL:(t + 1) * WCOL],
+                                 T.wb[:, t * 4 * WCOL:(t + 1) * 4 * WCOL]).then_inc(T.sem.qw, 1)
+    for t, sem in enumerate((T.sem.x0, T.sem.x1)):
+        g.vector.wait_ge(sem, 16)
+        g.vector.quantize_mx(T.xq[:, t * XCOL:(t + 1) * XCOL], T.xs[:, t * XCOL:(t + 1) * XCOL],
+                             T.xb[:, t * 4 * XCOL:(t + 1) * 4 * XCOL]).then_inc(T.sem.qx, 1)
+
+    if core == root:
+        lay = _root_engines(plan, topo)
+        g.wait_ge(T.sem.qw, KT)
+        g.remote_dma_fused([transfer("C", [plan["c_same"]], lay["c_same"]),
+                            transfer("C", [plan["c_other"]], lay["c_other"])], local_sem=T.sem.sent)
+        g.remote_dma_fused([transfer("S", [plan["s_same"]], lay["s_same"]),
+                            transfer("S", [plan["s_other"]], lay["s_other"]),
+                            transfer("S", [plan["s_near"]], lay["s_near"])], local_sem=T.sem.sent)
+        g.remote_dma_fused([transfer("C", plan["near"], lay["near"])], local_sem=T.sem.sent)
+        g.tensor.wait_ge(T.sem.qw, KT)
+    else:
+        senders = [s for s, (_, dsts) in plan["jobs"].items() if core in dsts]
+        if core in plan["near"]:
+            senders.append(root)
+        g.tensor.wait_ge(T.sem.arr, sum(len(_engines(topo.mask(s, core))) for s in senders))
+
+    g.tensor.wait_ge(T.sem.qx, KT)
+    for t in range(KT):
+        mm = g.tensor.matmul_mx(T.acc[:, 0:XCOL],
+                                T.wq[:, t * WCOL:(t + 1) * WCOL], T.ws[:, t * WCOL:(t + 1) * WCOL],
+                                T.xq[:, t * XCOL:(t + 1) * XCOL], T.xs[:, t * XCOL:(t + 1) * XCOL],
+                                t == 0, t == KT - 1)
+    mm.then_inc(T.sem.mm, 1)
+    g.vector.wait_ge(T.sem.mm, 1)
+    g.vector.tensor_copy(T.yb[:], T.acc[:, 0:XCOL]).then_inc(T.sem.cp, 1)
+    g.sync.wait_ge(T.sem.cp, 1)
+    g.sync.dma_start(T.y[:], T.yb[:]).then_inc(T.sem.st, 16)
+    g.sync.wait_ge(T.sem.st, 16)
+    if core == root:
+        g.wait_ge(T.sem.sent, sum(len(v) for v in _root_engines(plan, topo).values()))
+
+
+def _root_engines(plan, topo):
+    root = plan["root"]
+    on = _engines(topo.mask(root, plan["c_same"]))
+    off = _engines(topo.mask(root, plan["near"][0]))
+    stay = [e for e in on if e not in off]
+    return {
+        "c_same": on[0::2], "c_other": on[1::2],
+        "s_same": stay[0::2], "s_other": stay[1::2], "s_near": off,
+        "near": off,
+    }
+
+
+def _landing(plan, topo):
+    lay = _root_engines(plan, topo)
+    return {plan[k]: len(lay[k]) for k in ("c_same", "c_other", "s_same", "s_other", "s_near")}

@@ -1,9 +1,11 @@
 from concourse.bass import DstId, RemoteDMATransfer
-from concourse.mybir import dt
+from concourse.mybir import dt, ActivationFunctionType
 
 KT = 2
 WCOL = 128
 XCOL = 256
+HCOL = 128
+BANK = 512
 
 SCRATCH = {
     "wb": ("sbuf", [128, KT * 4 * WCOL], "bfloat16"),
@@ -12,10 +14,11 @@ SCRATCH = {
     "ws": ("sbuf", [128, KT * WCOL], "uint8"),
     "xq": ("sbuf", [128, KT * XCOL], "float8_e4m3fn_x4"),
     "xs": ("sbuf", [128, KT * XCOL], "uint8"),
-    "acc": ("psum", [128, 512], "float32"),
+    "acc": ("psum", [128, 2 * BANK], "float32"),
     "yb": ("sbuf", [128, XCOL], "float32"),
 }
-SEMAPHORES = ["w0", "w1", "x0", "x1", "qw", "qx", "arr", "sent", "mm", "cp", "st"]
+SEMAPHORES = ["w0", "w1", "x0", "x1", "qw0", "qw1", "qx", "arr", "arr1", "sent",
+              "mm0", "mm1", "cp0", "cp1", "st0", "st1"]
 
 
 def _engines(mask):
@@ -39,38 +42,55 @@ def _plan(cores, root_rank, topo):
     owners = [c for c in chipmates if all(topo.may_write(c, d) for d in far)]
     own_same = [c for c in owners if topo.die(c) == topo.die(root)]
     own_other = [c for c in owners if topo.die(c) != topo.die(root)]
+    plain_same = [c for c in chipmates if c not in owners and topo.die(c) == topo.die(root)]
     plain_other = [c for c in chipmates if c not in owners and topo.die(c) != topo.die(root)]
     half = len(far) // 2
     far_a, far_b = far[:half], far[half:]
     return {
-        "root": root, "near": near,
+        "root": root, "near": near, "direct": near[:-1],
         "c_same": own_same[0], "c_other": own_other[0],
         "s_same": own_same[1], "s_other": own_other[1],
         "s_near": plain_other[0],
+        "c_near": plain_same[0],
         "jobs": {
-            own_same[0]: ("C", far_a), own_other[0]: ("C", far_b),
-            own_same[1]: ("S", far_b), own_other[1]: ("S", far_a),
-            plain_other[0]: ("S", near),
+            own_same[0]: (("C0", "C1"), far_a), own_other[0]: (("C0", "C1"), far_b),
+            own_same[1]: (("S",), far_b), own_other[1]: (("S",), far_a),
+            plain_other[0]: (("S",), near), plain_same[0]: (("C",), near[-1:]),
         },
+    }
+
+
+def _root_engines(plan, topo):
+    root = plan["root"]
+    on = _engines(topo.mask(root, plan["c_same"]))
+    off = _engines(topo.mask(root, plan["near"][0]))
+    stay = [e for e in on if e not in off]
+    return {
+        "c_same": on[0::2], "c_other": on[1::2],
+        "s_same": stay[0::2], "s_other": stay[1::2], "s_near": off,
+        "direct": off, "c_near": stay,
     }
 
 
 def rank_program(g, core, T, topo):
     plan = _plan(T.cores, T.root, topo)
+    lay = _root_engines(plan, topo)
     root = plan["root"]
     rank = T.rank_of(core)
 
     def piece(kind):
-        if kind == "C":
-            return T.wq[:, 0:KT * WCOL].bitcast(dt.uint8)
-        return T.ws[:, 0:KT * WCOL]
+        if kind == "S":
+            return T.ws[:, 0:KT * WCOL]
+        a, b = {"C": (0, KT), "C0": (0, 1), "C1": (1, 2)}[kind]
+        return T.wq[:, a * WCOL:b * WCOL].bitcast(dt.uint8)
 
     def transfer(kind, dsts, engines):
         ids = []
         for d in dsts:
             rid, pid, _ = topo.addr(d)
             ids.append(DstId(rid=rid, pnc=pid))
-        return RemoteDMATransfer(dst_ids=ids, dma_engine_mask=_mask(engines), remote_sem=T.sem.arr,
+        return RemoteDMATransfer(dst_ids=ids, dma_engine_mask=_mask(engines),
+                                 remote_sem=T.sem.arr1 if kind == "C1" else T.sem.arr,
                                  srcs=[piece(kind)], dsts=[piece(kind) for _ in dsts])
 
     def common(src, dsts):
@@ -80,11 +100,13 @@ def rank_program(g, core, T, topo):
         return _engines(m)
 
     if core in plan["jobs"]:
-        kind, dsts = plan["jobs"][core]
+        kinds, dsts = plan["jobs"][core]
         eng = common(core, dsts)
-        g.wait_ge(T.sem.arr, _landing(plan, topo)[core])
-        g.remote_dma_fused([transfer(kind, dsts, eng)], local_sem=T.sem.sent)
-        g.wait_ge(T.sem.sent, len(eng))
+        landing = {plan[k]: len(lay[k]) for k in ("c_same", "c_other", "s_same", "s_other", "s_near", "c_near")}
+        for kind in kinds:
+            g.wait_ge(T.sem.arr1 if kind == "C1" else T.sem.arr, landing[core])
+            g.remote_dma_fused([transfer(kind, dsts, eng)], local_sem=T.sem.sent)
+        g.wait_ge(T.sem.sent, len(kinds) * len(eng))
         return
     if rank is None:
         return
@@ -96,59 +118,68 @@ def rank_program(g, core, T, topo):
     g.scalar.dma_start(T.xb[:, 4 * XCOL:8 * XCOL], T.x[:, 4 * XCOL:8 * XCOL]).then_inc(T.sem.x1, 16)
 
     if core == root:
-        for t, sem in enumerate((T.sem.w0, T.sem.w1)):
+        for t, (sem, done) in enumerate(((T.sem.w0, T.sem.qw0), (T.sem.w1, T.sem.qw1))):
             g.vector.wait_ge(sem, 16)
             g.vector.quantize_mx(T.wq[:, t * WCOL:(t + 1) * WCOL], T.ws[:, t * WCOL:(t + 1) * WCOL],
-                                 T.wb[:, t * 4 * WCOL:(t + 1) * 4 * WCOL]).then_inc(T.sem.qw, 1)
+                                 T.wb[:, t * 4 * WCOL:(t + 1) * 4 * WCOL]).then_inc(done, 1)
     for t, sem in enumerate((T.sem.x0, T.sem.x1)):
         g.vector.wait_ge(sem, 16)
         g.vector.quantize_mx(T.xq[:, t * XCOL:(t + 1) * XCOL], T.xs[:, t * XCOL:(t + 1) * XCOL],
                              T.xb[:, t * 4 * XCOL:(t + 1) * 4 * XCOL]).then_inc(T.sem.qx, 1)
 
+    second = None
     if core == root:
-        lay = _root_engines(plan, topo)
-        g.wait_ge(T.sem.qw, KT)
-        g.remote_dma_fused([transfer("C", [plan["c_same"]], lay["c_same"]),
-                            transfer("C", [plan["c_other"]], lay["c_other"])], local_sem=T.sem.sent)
+        g.wait_ge(T.sem.qw0, 1)
+        g.remote_dma_fused([transfer("C0", [plan["c_same"]], lay["c_same"]),
+                            transfer("C0", [plan["c_other"]], lay["c_other"])], local_sem=T.sem.sent)
+        g.wait_ge(T.sem.qw1, 1)
+        g.remote_dma_fused([transfer("C1", [plan["c_same"]], lay["c_same"]),
+                            transfer("C1", [plan["c_other"]], lay["c_other"])], local_sem=T.sem.sent)
         g.remote_dma_fused([transfer("S", [plan["s_same"]], lay["s_same"]),
                             transfer("S", [plan["s_other"]], lay["s_other"]),
                             transfer("S", [plan["s_near"]], lay["s_near"])], local_sem=T.sem.sent)
-        g.remote_dma_fused([transfer("C", plan["near"], lay["near"])], local_sem=T.sem.sent)
-        g.tensor.wait_ge(T.sem.qw, KT)
+        g.remote_dma_fused([transfer("C", plan["direct"], lay["direct"]),
+                            transfer("C", [plan["c_near"]], lay["c_near"])], local_sem=T.sem.sent)
+        g.tensor.wait_ge(T.sem.qw0, 1)
+        second = (T.sem.qw1, 1)
     else:
-        senders = [s for s, (_, dsts) in plan["jobs"].items() if core in dsts]
-        if core in plan["near"]:
-            senders.append(root)
-        g.tensor.wait_ge(T.sem.arr, sum(len(_engines(topo.mask(s, core))) for s in senders))
+        first, later = 0, 0
+        for s, (kinds, dsts) in plan["jobs"].items():
+            if core in dsts:
+                for kind in kinds:
+                    if kind == "C1":
+                        later += len(common(s, dsts))
+                    else:
+                        first += len(common(s, dsts))
+        if core in plan["direct"]:
+            first += len(lay["direct"])
+        g.tensor.wait_ge(T.sem.arr, first)
+        if later:
+            second = (T.sem.arr1, later)
 
     g.tensor.wait_ge(T.sem.qx, KT)
+    done = (T.sem.mm0, T.sem.mm1)
     for t in range(KT):
-        mm = g.tensor.matmul_mx(T.acc[:, 0:XCOL],
-                                T.wq[:, t * WCOL:(t + 1) * WCOL], T.ws[:, t * WCOL:(t + 1) * WCOL],
-                                T.xq[:, t * XCOL:(t + 1) * XCOL], T.xs[:, t * XCOL:(t + 1) * XCOL],
-                                t == 0, t == KT - 1)
-    mm.then_inc(T.sem.mm, 1)
-    g.vector.wait_ge(T.sem.mm, 1)
-    g.vector.tensor_copy(T.yb[:], T.acc[:, 0:XCOL]).then_inc(T.sem.cp, 1)
-    g.sync.wait_ge(T.sem.cp, 1)
-    g.sync.dma_start(T.y[:], T.yb[:]).then_inc(T.sem.st, 16)
-    g.sync.wait_ge(T.sem.st, 16)
+        if t == 1 and second is not None:
+            g.tensor.wait_ge(second[0], second[1])
+        for h in range(2):
+            a = t * XCOL + h * HCOL
+            mm = g.tensor.matmul_mx(T.acc[:, h * BANK:h * BANK + HCOL],
+                                    T.wq[:, t * WCOL:(t + 1) * WCOL], T.ws[:, t * WCOL:(t + 1) * WCOL],
+                                    T.xq[:, a:a + HCOL], T.xs[:, a:a + HCOL],
+                                    t == 0, t == KT - 1)
+            if t == KT - 1:
+                mm.then_inc(done[h], 1)
+    g.vector.wait_ge(T.sem.mm0, 1)
+    g.vector.tensor_copy(T.yb[:, 0:HCOL], T.acc[:, 0:HCOL]).then_inc(T.sem.cp0, 1)
+    g.sync.wait_ge(T.sem.cp0, 1)
+    g.sync.dma_start(T.y[:, 0:HCOL], T.yb[:, 0:HCOL]).then_inc(T.sem.st0, 16)
+    g.scalar.wait_ge(T.sem.mm1, 1)
+    g.scalar.activation(T.yb[:, HCOL:2 * HCOL], T.acc[:, BANK:BANK + HCOL],
+                        ActivationFunctionType.Copy).then_inc(T.sem.cp1, 1)
+    g.scalar.wait_ge(T.sem.cp1, 1)
+    g.scalar.dma_start(T.y[:, HCOL:2 * HCOL], T.yb[:, HCOL:2 * HCOL]).then_inc(T.sem.st1, 16)
+    g.sync.wait_ge(T.sem.st0, 16)
+    g.scalar.wait_ge(T.sem.st1, 16)
     if core == root:
-        g.wait_ge(T.sem.sent, sum(len(v) for v in _root_engines(plan, topo).values()))
-
-
-def _root_engines(plan, topo):
-    root = plan["root"]
-    on = _engines(topo.mask(root, plan["c_same"]))
-    off = _engines(topo.mask(root, plan["near"][0]))
-    stay = [e for e in on if e not in off]
-    return {
-        "c_same": on[0::2], "c_other": on[1::2],
-        "s_same": stay[0::2], "s_other": stay[1::2], "s_near": off,
-        "near": off,
-    }
-
-
-def _landing(plan, topo):
-    lay = _root_engines(plan, topo)
-    return {plan[k]: len(lay[k]) for k in ("c_same", "c_other", "s_same", "s_other", "s_near")}
+        g.wait_ge(T.sem.sent, sum(len(v) for v in lay.values()) + len(lay["c_same"]) + len(lay["c_other"]))

from concourse.bass import DstId, RemoteDMATransfer
from concourse.mybir import dt, ActivationFunctionType

KT = 2
WCOL = 128
XCOL = 256
HCOL = 128
BANK = 512

SCRATCH = {
    "wb": ("sbuf", [128, KT * 4 * WCOL], "bfloat16"),
    "xb": ("sbuf", [128, KT * 4 * XCOL], "bfloat16"),
    "wq": ("sbuf", [128, KT * WCOL], "float8_e4m3fn_x4"),
    "ws": ("sbuf", [128, KT * WCOL], "uint8"),
    "xq": ("sbuf", [128, KT * XCOL], "float8_e4m3fn_x4"),
    "xs": ("sbuf", [128, KT * XCOL], "uint8"),
    "acc": ("psum", [128, 2 * BANK], "float32"),
    "yb": ("sbuf", [128, XCOL], "float32"),
}
SEMAPHORES = ["w0", "w1", "x0", "x1", "qw0", "qw1", "qx", "arr", "arr1", "sent",
              "mm0", "mm1", "cp0", "cp1", "st0", "st1"]


def _engines(mask):
    return [e for e in range(mask.bit_length()) if (mask >> e) & 1]


def _mask(engines):
    m = 0
    for e in engines:
        m |= 1 << e
    return m


def _plan(cores, root_rank, topo):
    root = cores[root_rank]
    dests = [c for c in cores if c != root]
    near = [d for d in dests if topo.may_write(root, d)]
    far = [d for d in dests if not topo.may_write(root, d)]
    chipmates = [c for c in range(topo.CHIPS * topo.CORES_PER_CHIP)
                 if topo.chip(c) == topo.chip(root) and c != root and c not in cores]
    owners = [c for c in chipmates if all(topo.may_write(c, d) for d in far)]
    own_same = [c for c in owners if topo.die(c) == topo.die(root)]
    own_other = [c for c in owners if topo.die(c) != topo.die(root)]
    plain_same = [c for c in chipmates if c not in owners and topo.die(c) == topo.die(root)]
    plain_other = [c for c in chipmates if c not in owners and topo.die(c) != topo.die(root)]
    half = len(far) // 2
    far_a, far_b = far[:half], far[half:]
    return {
        "root": root, "near": near, "direct": near[:-1],
        "c_same": own_same[0], "c_other": own_other[0],
        "s_same": own_same[1], "s_other": own_other[1],
        "s_near": plain_other[0],
        "c_near": plain_same[0],
        "jobs": {
            own_same[0]: (("C0", "C1"), far_a), own_other[0]: (("C0", "C1"), far_b),
            own_same[1]: (("S",), far_b), own_other[1]: (("S",), far_a),
            plain_other[0]: (("S",), near), plain_same[0]: (("C",), near[-1:]),
        },
    }


def _root_engines(plan, topo):
    root = plan["root"]
    on = _engines(topo.mask(root, plan["c_same"]))
    off = _engines(topo.mask(root, plan["near"][0]))
    stay = [e for e in on if e not in off]
    return {
        "c_same": on[0::2], "c_other": on[1::2],
        "s_same": stay[0::2], "s_other": stay[1::2], "s_near": off,
        "direct": off, "c_near": stay,
    }


def rank_program(g, core, T, topo):
    plan = _plan(T.cores, T.root, topo)
    lay = _root_engines(plan, topo)
    root = plan["root"]
    rank = T.rank_of(core)

    def piece(kind):
        if kind == "S":
            return T.ws[:, 0:KT * WCOL]
        a, b = {"C": (0, KT), "C0": (0, 1), "C1": (1, 2)}[kind]
        return T.wq[:, a * WCOL:b * WCOL].bitcast(dt.uint8)

    def transfer(kind, dsts, engines):
        ids = []
        for d in dsts:
            rid, pid, _ = topo.addr(d)
            ids.append(DstId(rid=rid, pnc=pid))
        return RemoteDMATransfer(dst_ids=ids, dma_engine_mask=_mask(engines),
                                 remote_sem=T.sem.arr1 if kind == "C1" else T.sem.arr,
                                 srcs=[piece(kind)], dsts=[piece(kind) for _ in dsts])

    def common(src, dsts):
        m = topo.mask(src, dsts[0])
        for d in dsts[1:]:
            m &= topo.mask(src, d)
        return _engines(m)

    if core in plan["jobs"]:
        kinds, dsts = plan["jobs"][core]
        eng = common(core, dsts)
        landing = {plan[k]: len(lay[k]) for k in ("c_same", "c_other", "s_same", "s_other", "s_near", "c_near")}
        for kind in kinds:
            g.wait_ge(T.sem.arr1 if kind == "C1" else T.sem.arr, landing[core])
            g.remote_dma_fused([transfer(kind, dsts, eng)], local_sem=T.sem.sent)
        g.wait_ge(T.sem.sent, len(kinds) * len(eng))
        return
    if rank is None:
        return

    if core == root:
        g.sync.dma_start(T.wb[:, 0:4 * WCOL], T.w[:, 0:4 * WCOL]).then_inc(T.sem.w0, 16)
        g.scalar.dma_start(T.wb[:, 4 * WCOL:8 * WCOL], T.w[:, 4 * WCOL:8 * WCOL]).then_inc(T.sem.w1, 16)
    g.sync.dma_start(T.xb[:, 0:4 * XCOL], T.x[:, 0:4 * XCOL]).then_inc(T.sem.x0, 16)
    g.scalar.dma_start(T.xb[:, 4 * XCOL:8 * XCOL], T.x[:, 4 * XCOL:8 * XCOL]).then_inc(T.sem.x1, 16)

    if core == root:
        for t, (sem, done) in enumerate(((T.sem.w0, T.sem.qw0), (T.sem.w1, T.sem.qw1))):
            g.vector.wait_ge(sem, 16)
            g.vector.quantize_mx(T.wq[:, t * WCOL:(t + 1) * WCOL], T.ws[:, t * WCOL:(t + 1) * WCOL],
                                 T.wb[:, t * 4 * WCOL:(t + 1) * 4 * WCOL]).then_inc(done, 1)
    for t, sem in enumerate((T.sem.x0, T.sem.x1)):
        g.vector.wait_ge(sem, 16)
        g.vector.quantize_mx(T.xq[:, t * XCOL:(t + 1) * XCOL], T.xs[:, t * XCOL:(t + 1) * XCOL],
                             T.xb[:, t * 4 * XCOL:(t + 1) * 4 * XCOL]).then_inc(T.sem.qx, 1)

    second = None
    if core == root:
        g.wait_ge(T.sem.qw0, 1)
        g.remote_dma_fused([transfer("C0", [plan["c_same"]], lay["c_same"]),
                            transfer("C0", [plan["c_other"]], lay["c_other"])], local_sem=T.sem.sent)
        g.wait_ge(T.sem.qw1, 1)
        g.remote_dma_fused([transfer("C1", [plan["c_same"]], lay["c_same"]),
                            transfer("C1", [plan["c_other"]], lay["c_other"])], local_sem=T.sem.sent)
        g.remote_dma_fused([transfer("S", [plan["s_same"]], lay["s_same"]),
                            transfer("S", [plan["s_other"]], lay["s_other"]),
                            transfer("S", [plan["s_near"]], lay["s_near"])], local_sem=T.sem.sent)
        g.remote_dma_fused([transfer("C", plan["direct"], lay["direct"]),
                            transfer("C", [plan["c_near"]], lay["c_near"])], local_sem=T.sem.sent)
        g.tensor.wait_ge(T.sem.qw0, 1)
        second = (T.sem.qw1, 1)
    else:
        first, later = 0, 0
        for s, (kinds, dsts) in plan["jobs"].items():
            if core in dsts:
                for kind in kinds:
                    if kind == "C1":
                        later += len(common(s, dsts))
                    else:
                        first += len(common(s, dsts))
        if core in plan["direct"]:
            first += len(lay["direct"])
        g.tensor.wait_ge(T.sem.arr, first)
        if later:
            second = (T.sem.arr1, later)

    g.tensor.wait_ge(T.sem.qx, KT)
    done = (T.sem.mm0, T.sem.mm1)
    for t in range(KT):
        if t == 1 and second is not None:
            g.tensor.wait_ge(second[0], second[1])
        for h in range(2):
            a = t * XCOL + h * HCOL
            mm = g.tensor.matmul_mx(T.acc[:, h * BANK:h * BANK + HCOL],
                                    T.wq[:, t * WCOL:(t + 1) * WCOL], T.ws[:, t * WCOL:(t + 1) * WCOL],
                                    T.xq[:, a:a + HCOL], T.xs[:, a:a + HCOL],
                                    t == 0, t == KT - 1)
            if t == KT - 1:
                mm.then_inc(done[h], 1)
    g.vector.wait_ge(T.sem.mm0, 1)
    g.vector.tensor_copy(T.yb[:, 0:HCOL], T.acc[:, 0:HCOL]).then_inc(T.sem.cp0, 1)
    g.sync.wait_ge(T.sem.cp0, 1)
    g.sync.dma_start(T.y[:, 0:HCOL], T.yb[:, 0:HCOL]).then_inc(T.sem.st0, 16)
    g.scalar.wait_ge(T.sem.mm1, 1)
    g.scalar.activation(T.yb[:, HCOL:2 * HCOL], T.acc[:, BANK:BANK + HCOL],
                        ActivationFunctionType.Copy).then_inc(T.sem.cp1, 1)
    g.scalar.wait_ge(T.sem.cp1, 1)
    g.scalar.dma_start(T.y[:, HCOL:2 * HCOL], T.yb[:, HCOL:2 * HCOL]).then_inc(T.sem.st1, 16)
    g.sync.wait_ge(T.sem.st0, 16)
    g.scalar.wait_ge(T.sem.st1, 16)
    if core == root:
        g.wait_ge(T.sem.sent, sum(len(v) for v in lay.values()) + len(lay["c_same"]) + len(lay["c_other"]))
